import numpy as np
import ml_dtypes

BF16 = ml_dtypes.bfloat16


def bf(x):
    return np.asarray(x, np.float32).astype(BF16)


def f32(x):
    return np.asarray(x, np.float32)


def f64(x):
    return np.asarray(x).astype(np.float64)


def striped(idx):
    return np.tile(idx.reshape(-1, 16).T, (8, 1))


def rows(idx, k):
    return np.tile(idx, (k, 1))


def look(tab, idx):
    return np.take_along_axis(f64(tab), rows(idx, len(tab)), axis=1)


K, S, V, N = 512, 2048, 512, 512


def setup_inputs():
    return {"tab": f32(np.random.standard_normal((2, K, S))), "y": f32(np.random.standard_normal((K, V))), "offs": striped(np.random.permutation(S)[:N])}


def reference(tab, y, offs):
    idx = offs[:16].T.reshape(-1)
    x = (look(tab[0], idx) + f64(y)) * (np.maximum(look(tab[1], idx), 0.0))
    return x

@@ -1,0 +1,44 @@
+import concourse.mybir as mybir
+
+F32 = mybir.dt.float32
+U16 = mybir.dt.uint16
+ADD = mybir.AluOpType.add
+MULT = mybir.AluOpType.mult
+RELU = mybir.ActivationFunctionType.Relu
+
+ROWS, PLACES, PICKS = 512, 2048, 512
+PART = 128
+BLOCKS = ROWS // PART
+
+FLOPS = 3 * ROWS * PICKS
+
+
+def tile_lookup_vg_addrelu_out_kernel(tc, tab, y, offs, out):
+    nc = tc.nc
+    with (
+        tc.tile_pool(name="listing", bufs=1) as listing,
+        tc.tile_pool(name="windows", bufs=BLOCKS) as windows,
+        tc.tile_pool(name="work", bufs=BLOCKS) as work,
+    ):
+        offsets = listing.tile([PART, PICKS // 16], U16)
+        nc.sync.dma_start(offsets[:], offs)
+
+        for b in range(BLOCKS):
+            rows = slice(b * PART, (b + 1) * PART)
+
+            gates = windows.tile([PART, PLACES], F32)
+            stream = work.tile([PART, PICKS], F32)
+            values = windows.tile([PART, PLACES], F32)
+            nc.sync.dma_start(gates[:], tab[1, rows, :])
+            nc.sync.dma_start(stream[:], y[rows, :])
+            nc.sync.dma_start(values[:], tab[0, rows, :])
+
+            opened = work.tile([PART, PICKS], F32)
+            nc.scalar.activation(opened[:], gates[:].indirect(offsets[:]), RELU)
+
+            summed = work.tile([PART, PICKS], F32)
+            nc.vector.tensor_tensor(summed[:], values[:].indirect(offsets[:]), stream[:], ADD)
+
+            result = work.tile([PART, PICKS], F32)
+            nc.vector.tensor_tensor(result[:], summed[:], opened[:], MULT)
+            nc.sync.dma_start(out[rows, :], result[:])

@@ -23,22 +23,23 @@ def tile_lookup_vg_addrelu_out_kernel(tc, tab, y, offs, out):
         offsets = listing.tile([PART, PICKS // 16], U16)
         nc.sync.dma_start(offsets[:], offs)
 
+        gates, streams, values = [], [], []
         for b in range(BLOCKS):
             rows = slice(b * PART, (b + 1) * PART)
+            gates.append(windows.tile([PART, PLACES], F32, name="gate_window"))
+            streams.append(work.tile([PART, PICKS], F32, name="stream"))
+            values.append(windows.tile([PART, PLACES], F32, name="value_window"))
+            nc.sync.dma_start(gates[b][:], tab[1, rows, :])
+            nc.sync.dma_start(streams[b][:], y[rows, :])
+            nc.sync.dma_start(values[b][:], tab[0, rows, :])
 
-            gates = windows.tile([PART, PLACES], F32)
-            stream = work.tile([PART, PICKS], F32)
-            values = windows.tile([PART, PLACES], F32)
-            nc.sync.dma_start(gates[:], tab[1, rows, :])
-            nc.sync.dma_start(stream[:], y[rows, :])
-            nc.sync.dma_start(values[:], tab[0, rows, :])
-
+        for b in range(BLOCKS):
             opened = work.tile([PART, PICKS], F32)
-            nc.scalar.activation(opened[:], gates[:].indirect(offsets[:]), RELU)
+            nc.scalar.activation(opened[:], gates[b][:].indirect(offsets[:]), RELU)
 
             summed = work.tile([PART, PICKS], F32)
-            nc.vector.tensor_tensor(summed[:], values[:].indirect(offsets[:]), stream[:], ADD)
+            nc.vector.tensor_tensor(summed[:], values[b][:].indirect(offsets[:]), streams[b][:], ADD)
 
             result = work.tile([PART, PICKS], F32)
             nc.vector.tensor_tensor(result[:], summed[:], opened[:], MULT)
-            nc.sync.dma_start(out[rows, :], result[:])
+            nc.sync.dma_start(out[b * PART : (b + 1) * PART, :], result[:])

@@ -15,31 +15,40 @@ FLOPS = 3 * ROWS * PICKS
 
 def tile_lookup_vg_addrelu_out_kernel(tc, tab, y, offs, out):
     nc = tc.nc
+    value_rows = tab[0].rearrange("(p b) s -> b p s", b=BLOCKS)
+    gate_rows = tab[1].rearrange("(p b) s -> b p s", b=BLOCKS)
+    out_rows = out.rearrange("(p b) j -> b p j", b=BLOCKS)
     with (
         tc.tile_pool(name="listing", bufs=1) as listing,
         tc.tile_pool(name="windows", bufs=BLOCKS) as windows,
-        tc.tile_pool(name="work", bufs=BLOCKS) as work,
+        tc.tile_pool(name="work", bufs=BLOCKS + 1) as work,
     ):
         offsets = listing.tile([PART, PICKS // 16], U16)
         nc.sync.dma_start(offsets[:], offs)
 
-        gates, streams, values = [], [], []
+        gates = [windows.tile([PART, PLACES], F32, name="gate_window") for b in range(BLOCKS)]
+        values = [windows.tile([PART, PLACES], F32, name="value_window") for b in range(BLOCKS)]
+        stream = listing.tile([PART, BLOCKS * PICKS], F32)
         for b in range(BLOCKS):
-            rows = slice(b * PART, (b + 1) * PART)
-            gates.append(windows.tile([PART, PLACES], F32, name="gate_window"))
-            streams.append(work.tile([PART, PICKS], F32, name="stream"))
-            values.append(windows.tile([PART, PLACES], F32, name="value_window"))
-            nc.sync.dma_start(gates[b][:], tab[1, rows, :])
-            nc.sync.dma_start(streams[b][:], y[rows, :])
-            nc.sync.dma_start(values[b][:], tab[0, rows, :])
+            nc.sync.dma_start(gates[b][:], gate_rows[b])
+            if b == 0:
+                nc.sync.dma_start(stream[:], y.rearrange("(p b) j -> p (b j)", b=BLOCKS))
+            nc.sync.dma_start(values[b][:], value_rows[b])
 
         for b in range(BLOCKS):
             opened = work.tile([PART, PICKS], F32)
             nc.scalar.activation(opened[:], gates[b][:].indirect(offsets[:]), RELU)
 
-            summed = work.tile([PART, PICKS], F32)
-            nc.vector.tensor_tensor(summed[:], values[b][:].indirect(offsets[:]), streams[b][:], ADD)
+            pieces = 2 if b == BLOCKS - 1 else 1
+            width = PICKS // pieces
+            for start in range(0, PICKS, width):
+                picks = slice(start, start + width)
+                listed = offsets[:, start // 16 : (start + width) // 16]
+                added = stream[:, b * PICKS + start : b * PICKS + start + width]
 
-            result = work.tile([PART, PICKS], F32)
-            nc.vector.tensor_tensor(result[:], summed[:], opened[:], MULT)
-            nc.sync.dma_start(out[b * PART : (b + 1) * PART, :], result[:])
+                summed = work.tile([PART, width], F32)
+                nc.vector.tensor_tensor(summed[:], values[b][:].indirect(listed), added, ADD)
+
+                result = work.tile([PART, width], F32)
+                nc.vector.tensor_tensor(result[:], summed[:], opened[:, picks], MULT)
+                nc.sync.dma_start(out_rows[b][:, picks], result[:])

import concourse.mybir as mybir

F32 = mybir.dt.float32
U16 = mybir.dt.uint16
ADD = mybir.AluOpType.add
MULT = mybir.AluOpType.mult
RELU = mybir.ActivationFunctionType.Relu

ROWS, PLACES, PICKS = 512, 2048, 512
PART = 128
BLOCKS = ROWS // PART

FLOPS = 3 * ROWS * PICKS


def tile_lookup_vg_addrelu_out_kernel(tc, tab, y, offs, out):
    nc = tc.nc
    value_rows = tab[0].rearrange("(p b) s -> b p s", b=BLOCKS)
    gate_rows = tab[1].rearrange("(p b) s -> b p s", b=BLOCKS)
    out_rows = out.rearrange("(p b) j -> b p j", b=BLOCKS)
    with (
        tc.tile_pool(name="listing", bufs=1) as listing,
        tc.tile_pool(name="windows", bufs=BLOCKS) as windows,
        tc.tile_pool(name="work", bufs=BLOCKS + 1) as work,
    ):
        offsets = listing.tile([PART, PICKS // 16], U16)
        nc.sync.dma_start(offsets[:], offs)

        gates = [windows.tile([PART, PLACES], F32, name="gate_window") for b in range(BLOCKS)]
        values = [windows.tile([PART, PLACES], F32, name="value_window") for b in range(BLOCKS)]
        stream = listing.tile([PART, BLOCKS * PICKS], F32)
        for b in range(BLOCKS):
            nc.sync.dma_start(gates[b][:], gate_rows[b])
            if b == 0:
                nc.sync.dma_start(stream[:], y.rearrange("(p b) j -> p (b j)", b=BLOCKS))
            nc.sync.dma_start(values[b][:], value_rows[b])

        for b in range(BLOCKS):
            opened = work.tile([PART, PICKS], F32)
            nc.scalar.activation(opened[:], gates[b][:].indirect(offsets[:]), RELU)

            pieces = 2 if b == BLOCKS - 1 else 1
            width = PICKS // pieces
            for start in range(0, PICKS, width):
                picks = slice(start, start + width)
                listed = offsets[:, start // 16 : (start + width) // 16]
                added = stream[:, b * PICKS + start : b * PICKS + start + width]

                summed = work.tile([PART, width], F32)
                nc.vector.tensor_tensor(summed[:], values[b][:].indirect(listed), added, ADD)

                result = work.tile([PART, width], F32)
                nc.vector.tensor_tensor(result[:], summed[:], opened[:, picks], MULT)
                nc.sync.dma_start(out_rows[b][:, picks], result[:])
